import numpy as np
import ml_dtypes


def mxq(x, axis, fmt="e4m3"):
    dtype, down = {"e4m3": (ml_dtypes.float8_e4m3fn, 7), "e5m2": (ml_dtypes.float8_e5m2, 14)}[fmt]
    v = np.moveaxis(np.asarray(x, np.float32).astype(ml_dtypes.bfloat16).astype(np.float64), axis, -1)
    blocks = v.reshape(v.shape[:-1] + (-1, 32))
    amax = np.abs(blocks).max(-1, keepdims=True)
    byte = np.maximum(np.where(amax > 0, np.frexp(amax)[1] - 1 + 127, 0) - down, 1)
    scale = np.exp2(byte - 127.0)
    codes = (blocks / scale).astype(np.float32).astype(dtype).astype(np.float64)
    return np.moveaxis((codes * scale).reshape(v.shape), -1, axis)


WIDE = False


def mx_kscale(k):
    if not WIDE:
        return np.ones(k)
    levels = np.array([30, -30])
    if k % 512:
        return np.exp2(np.random.permutation(np.resize(levels, k // 32))).repeat(32)
    a = np.empty((k // 512, 16))
    for p in range(k // 512):
        a[p, :8] = np.random.permutation(np.resize(levels, 8))
        for g in range(8):
            far = levels[np.abs(levels - a[p, g]) >= 10]
            a[p, g + 8] = far[np.random.randint(len(far))]
    return np.exp2(a.ravel()).repeat(32)


BF16 = ml_dtypes.bfloat16


def bf(x):
    return np.asarray(x, np.float32).astype(BF16)


def f64(x):
    return np.asarray(x).astype(np.float64)


E2M1 = np.array([0.0, 0.5, 1.0, 1.5, 2.0, 3.0, 4.0, 6.0, -0.0, -0.5, -1.0, -1.5, -2.0, -3.0, -4.0, -6.0])


def pack_weight(w, fmt):
    k, n = w.shape
    w = f64(bf(w)).reshape(k // 32, 32, n)
    amax = np.abs(w).max(1)
    if fmt in ("e4m3", "e5m2"):
        byte = np.frexp(amax)[1] - 1 + 127 - (7 if fmt == "e4m3" else 14)
    else:
        mant, ex = np.frexp(amax / 6.0)
        byte = np.where(mant > 0.5, ex, ex - 1) + 127
    byte = np.clip(np.where(amax > 0, byte, 1), 1, 254)
    scaled = (w * np.exp2(127.0 - byte)[:, None, :]).reshape(k, n).astype(np.float32)
    by_word = np.ascontiguousarray(scaled.reshape(k // 512, 128, 4, n).transpose(0, 1, 3, 2))
    if fmt in ("e4m3", "e5m2"):
        words = by_word.astype(ml_dtypes.float8_e4m3fn if fmt == "e4m3" else ml_dtypes.float8_e5m2).view(np.uint8)
    else:
        c = by_word.astype(ml_dtypes.float4_e2m1fn).view(np.uint8) & 0xF
        words = c[..., 0::2] | (c[..., 1::2] << 4)
    return np.ascontiguousarray(words), np.ascontiguousarray(byte.astype(np.uint8).reshape(k // 512, 16, n))


def unpack_weight(words, scales, fmt):
    g, p, n, _ = words.shape
    if fmt in ("e4m3", "e5m2"):
        vals = np.ascontiguousarray(words).view(ml_dtypes.float8_e4m3fn if fmt == "e4m3" else ml_dtypes.float8_e5m2).astype(np.float64)
    else:
        nib = np.empty((g, p, n, 4), np.uint8)
        nib[..., 0::2] = words & 0xF
        nib[..., 1::2] = words >> 4
        vals = E2M1[nib]
    vals = vals * np.repeat(np.exp2(scales.astype(np.float64) - 127.0), 8, axis=1)[..., None]
    return vals.transpose(0, 1, 3, 2).reshape(g * 512, n)

def planes(Y):
    n, m = Y.shape
    b = f64(bf(Y)).reshape(n // 32, 32, m)
    amax = np.abs(b).max(1)
    byte = np.clip(np.where(amax > 0, np.frexp(amax)[1] - 1 + 127 - 7, 1), 1, 254)
    codes = (b * np.exp2(127.0 - byte)[:, None, :]).reshape(n, m).astype(np.float32).astype(ml_dtypes.float8_e4m3fn).view(np.uint8)
    words = codes.reshape(n // 512, 128, 4, m).transpose(0, 1, 3, 2)
    return np.ascontiguousarray(words), np.ascontiguousarray(byte.astype(np.uint8).reshape(n // 512, 16, m))


S, B, C, E, AX, K, N = 1024, 256, 512, 4, 3, 2048, 1536
MU, TAIL, REACH, SPREAD = 0.6, 1.2, 0.7, 0.8

def unit(v):
    return v / np.sqrt((v * v).sum(-1, keepdims=True))

def grasp_matrices_t():
    normal = unit(np.random.randn(C, B, AX))
    side = unit(np.cross(normal, np.random.randn(C, B, AX)))
    up = np.cross(normal, side)
    site = REACH * np.random.randn(C, B, AX)
    angle = (2 * np.pi * np.arange(E) / E).reshape(E, 1, 1)
    edge = unit(normal[:, None] + MU * (np.cos(angle) * side[:, None] + np.sin(angle) * up[:, None]))
    torque = np.cross(site[:, None], edge)
    return np.concatenate([edge, torque], axis=-1).reshape(K, N) / np.sqrt(K / AX)

def setup_inputs():
    s = mx_kscale(K)
    force = np.exp(TAIL * np.random.randn(K, S) - TAIL * TAIL)
    force_words, force_scales = pack_weight(force * s[:, None], "e5m2")
    grasp_t = bf(grasp_matrices_t() / s[:, None])
    wrench = bf(np.random.randn(S, N))
    weight = bf(np.exp(SPREAD * np.random.randn(N)))
    return {"force_words": force_words, "force_scales": force_scales, "grasp_t": grasp_t, "wrench": wrench, "weight": weight}

def reference(force_words, force_scales, grasp_t, wrench, weight):
    F = unpack_weight(force_words, force_scales, "e5m2")
    A = mxq(f64(grasp_t), 0, "e4m3")
    r = (F.T @ A) - f64(wrench)
    y = f64(weight) * np.square(r)
    Y = y.T
    words, scales = planes(Y)
    return y, words, scales

@@ -1,0 +1,314 @@
+from contextlib import ExitStack
+
+import concourse.mybir as mybir
+from concourse.masks import make_identity
+
+S, K, N = 1024, 2048, 1536
+FLOPS = 2 * S * K * N
+
+F32 = mybir.dt.float32
+BF16 = mybir.dt.bfloat16
+I32 = mybir.dt.int32
+U32 = mybir.dt.uint32
+U8 = mybir.dt.uint8
+E4M3X4 = mybir.dt.float8_e4m3fn_x4
+E5M2X4 = mybir.dt.float8_e5m2_x4
+ALU = mybir.AluOpType
+ACT = mybir.ActivationFunctionType
+
+P = 128
+PACK = 4
+K_PASS = P * PACK
+PASSES = K // K_PASS
+N_TILE = 512
+GROUPS = N // N_TILE
+S_TILES = S // P
+F_CHUNK = 2 * P
+PIECES = GROUPS * PASSES
+HEAD_PIECES = PASSES + 1
+ACC_BANKS = 4
+TURN_BANKS = 2
+RING = 3
+VECTOR_COLS_HEAD = 256
+VECTOR_COLS_LOOP = 288
+VECTOR_COLS_LAST = 336
+GPSIMD_COLS = 384
+LOOP_V = 0
+G_FIRST = 208
+GR0 = 7
+QLATE = 1
+SQFIRST = 20
+LAST_EARLY = 0
+WARM = 5
+A_RING = 3
+PEORDER = 0
+TAILV = 2
+
+
+def tile_grasp_wrench_residual_k2_kernel(
+    tc, force_words, force_scales, grasp_t, wrench, weight, out_0, out_1, out_2
+):
+    nc = tc.nc
+
+    units = [(g, j, 2) for g in range(GROUPS) for j in range(0, S_TILES, 2)]
+    units = units[:-1] + [(GROUPS - 1, S_TILES - 2, 1), (GROUPS - 1, S_TILES - 1, 1)]
+
+    with ExitStack() as ctx:
+        sb = ctx.enter_context(tc.tile_pool(name="sb", bufs=1))
+        ps = ctx.enter_context(tc.psum_pool(name="ps", bufs=1))
+        ctx.enter_context(tc.manual_schedule())
+
+        def tiles(pool, name, count, shape, dtype):
+            return [pool.tile(shape, dtype, name="%s%d" % (name, i), align_bytes=64) for i in range(count)]
+
+        def banks(name, count, shape):
+            return [ps.tile(shape, F32, name="%s%d" % (name, i)) for i in range(count)]
+
+        f_scales = sb.tile([P, PASSES, S], U8, name="f_scales", align_bytes=64)
+        f_words = tiles(sb, "f_words", S // F_CHUNK, [P, PASSES, F_CHUNK], U32)
+        a_raw = tiles(sb, "a_raw", PIECES, [P, PACK, N_TILE], BF16)
+        a_grouped = tiles(sb, "a_grouped", PASSES, [P, N_TILE * PACK], BF16)
+        a_codes = tiles(sb, "a_codes", PIECES, [P, N_TILE], U32)
+        a_scales = tiles(sb, "a_scales", PIECES, [P, N_TILE], U8)
+        wrench_sb = [sb.tile([P, cnt, N_TILE], BF16, name="wrench%d" % i, align_bytes=64) for i, (g, j, cnt) in enumerate(units)]
+        y_sb = [sb.tile([P, cnt * N_TILE], F32, name="y%d" % i, align_bytes=64) for i, (g, j, cnt) in enumerate(units)]
+        r_sb = tiles(sb, "r", RING, [P, 2 * N_TILE], F32)
+        y_half = tiles(sb, "y_half", RING, [P, 2 * N_TILE], BF16)
+        y_turned = tiles(sb, "y_turned", RING, [P, 2 * N_TILE], BF16)
+        y_codes = tiles(sb, "y_codes", GROUPS, [P, S], U32)
+        y_scales = tiles(sb, "y_scales", GROUPS, [P, S], U8)
+        weight_row = sb.tile([P, N], BF16, name="weight_row", align_bytes=64)
+        ones_src = sb.tile([P, P], BF16, name="ones_src", align_bytes=64)
+        ones = sb.tile([P, P], BF16, name="ones", align_bytes=64)
+        ident = sb.tile([P, P], F32, name="ident", align_bytes=64)
+        acc = banks("acc", ACC_BANKS, [P, N_TILE])
+        turn = banks("turn", TURN_BANKS, [P, N_TILE])
+        weight_bank = banks("weight_bank", 2, [P, N_TILE])
+
+        def load_a(c):
+            g, k = divmod(c, PASSES)
+            rows = grasp_t[k * K_PASS : (k + 1) * K_PASS, g * N_TILE : (g + 1) * N_TILE]
+            nc.sync.dma_start(out=a_raw[c][:], in_=rows.rearrange("(p t) n -> p t n", t=PACK))
+
+        def load_f(q):
+            src = force_words.rearrange("k p s t -> p k (s t)")[:, :, q * F_CHUNK * PACK : (q + 1) * F_CHUNK * PACK]
+            nc.sync.dma_start(out=f_words[q][:].bitcast(I32), in_=src.bitcast(I32))
+
+        def load_wrench(u):
+            g, j, cnt = units[u]
+            rows = wrench[j * P : (j + cnt) * P, g * N_TILE : (g + 1) * N_TILE]
+            nc.sync.dma_start(out=wrench_sb[u][:], in_=rows.rearrange("(j p) n -> p j n", p=P))
+
+        nc.vector.memset(f_scales[:].rearrange("p k s -> p (k s)").bitcast(I32), 0)
+        nc.vector.memset(weight_row[:].bitcast(I32), 0)
+        nc.vector.memset(ones_src[:], 1.0)
+        make_identity(nc, ident[:])
+
+        for c in range(PASSES):
+            load_a(c)
+        for quad in range(4):
+            nc.sync.dma_start(
+                out=f_scales[32 * quad : 32 * quad + 4, :, :].bitcast(I32),
+                in_=force_scales[:, 4 * quad : 4 * quad + 4, :].rearrange("k r s -> r k s").bitcast(I32),
+            )
+        nc.scalar.activation(out=ones[:], in_=ones_src[:], func=ACT.Square)
+        load_f(0)
+        load_wrench(0)
+        nc.sync.dma_start(out=weight_row[0:1, :], in_=weight.rearrange("(o n) -> o n", o=1))
+        for u in range(1, len(units)):
+            if u < S // F_CHUNK:
+                load_f(u)
+            if u == 1:
+                load_a(PASSES)
+            load_wrench(u)
+            if u + PASSES < PIECES:
+                load_a(u + PASSES)
+
+        def interleave(engine_copy, c, lo, hi):
+            dst = a_grouped[min(c, PASSES - 1)][:, lo * PACK : hi * PACK].rearrange("p (c i t) -> p c t i", i=4, t=PACK)
+            src = a_raw[c][:, :, lo:hi].rearrange("p t (c i) -> p c t i", i=4)
+            engine_copy(out=dst, in_=src)
+
+        def interleave_vector(c, split):
+            interleave(nc.vector.tensor_copy, c, 0, split)
+
+        def interleave_scalar(c, split, end=N_TILE):
+            interleave(nc.scalar.copy, c, split, end)
+
+        def interleave_gpsimd(c, lo):
+            nc.gpsimd.tensor_scalar(
+                out=a_grouped[min(c, PASSES - 1)][:, lo * PACK :].rearrange("p (c t) -> p c t", t=PACK),
+                in0=a_raw[c][:, :, lo:].rearrange("p t c -> p c t"),
+                scalar1=1.0, scalar2=0.0, op0=ALU.mult, op1=ALU.add,
+            )
+
+        def quantize_a(c):
+            nc.vector.quantize_mx(out=a_codes[c][:].bitcast(E4M3X4), scales=a_scales[c][:], in_=a_grouped[min(c, PASSES - 1)][:])
+
+        first_tile = [sum(cnt for g, j, cnt in units[:u]) for u in range(len(units))]
+
+        def mx_pass(u, jj, k):
+            g, j, cnt = units[u]
+            q, off = divmod((j + jj) * P, F_CHUNK)
+            nc.tensor.matmul_mx(
+                out=acc[(first_tile[u] + jj) % ACC_BANKS][:],
+                lhsT=f_words[q][:, k, off : off + P].bitcast(E5M2X4),
+                lhsT_scale=f_scales[:, k, (j + jj) * P : (j + jj + 1) * P],
+                rhs=a_codes[g * PASSES + k][:].bitcast(E4M3X4),
+                rhs_scale=a_scales[g * PASSES + k][:],
+                start=(k == 0),
+                stop=(k == PASSES - 1),
+            )
+
+        def product(u, passes=range(PASSES)):
+            if u > 0 and units[u][1] == 0:
+                for k in passes:
+                    for jj in range(units[u][2]):
+                        mx_pass(u, jj, k)
+            else:
+                for jj in range(units[u][2]):
+                    for k in passes:
+                        mx_pass(u, jj, k)
+
+        def spread_weight(g):
+            nc.tensor.matmul(
+                out=weight_bank[g % 2][:], lhsT=ones[:], rhs=weight_row[:, g * N_TILE : (g + 1) * N_TILE], start=True, stop=True
+            )
+
+        def subtract(u):
+            for jj in range(units[u][2]):
+                nc.vector.tensor_tensor(
+                    out=r_sb[u % RING][:, jj * N_TILE : (jj + 1) * N_TILE],
+                    in0=acc[(first_tile[u] + jj) % ACC_BANKS][:],
+                    in1=wrench_sb[u][:, jj, :],
+                    op=ALU.subtract,
+                )
+
+        def square(u):
+            width = units[u][2] * N_TILE
+            nc.scalar.activation(out=y_sb[u][:], in_=r_sb[u % RING][:, :width], func=ACT.Square)
+
+        def weigh(u):
+            g, j, cnt = units[u]
+            y3 = y_sb[u][:].rearrange("p (j n) -> p j n", j=cnt)
+            nc.vector.tensor_tensor(
+                out=y3, in0=y3, in1=weight_bank[g % 2][:].unsqueeze(1).to_broadcast([P, cnt, N_TILE]), op=ALU.mult
+            )
+            rows = out_0[j * P : (j + cnt) * P, g * N_TILE : (g + 1) * N_TILE]
+            nc.sync.dma_start(out=rows.rearrange("(j p) n -> p j n", p=P), in_=y3)
+
+        def gpsimd_copy(out, in_):
+            nc.gpsimd.tensor_scalar(out=out, in0=in_, scalar1=1.0, scalar2=0.0, op0=ALU.mult, op1=ALU.add)
+
+        def round_y(u, engine_copy, halves=slice(0, 2)):
+            width = units[u][2] * N_TILE
+            engine_copy(
+                out=y_half[u % RING][:, :width].rearrange("p (h m e) -> p h m e", h=2, e=2)[:, halves],
+                in_=y_sb[u][:].rearrange("p (m h e) -> p h m e", h=2, e=2)[:, halves],
+            )
+
+        def turn_y(u):
+            cnt = units[u][2]
+            words = y_half[u % RING][:, : cnt * N_TILE].bitcast(F32)
+            for b in range(2 * cnt):
+                nc.tensor.transpose(turn[u % TURN_BANKS][:, b * P : (b + 1) * P], words[:, b * P : (b + 1) * P], ident[:])
+
+        def copy_turned(u):
+            cnt = units[u][2]
+            nc.scalar.copy(
+                out=y_turned[u % RING][:, : cnt * N_TILE].bitcast(F32).rearrange("p (m h) -> p m h", h=2),
+                in_=turn[u % TURN_BANKS][:, : 2 * cnt * P].rearrange("p (h m) -> p m h", h=2),
+            )
+
+        def store_planes(g, lo, hi):
+            nc.sync.dma_start(
+                out=out_1[g].rearrange("p m t -> p (m t)")[:, lo * PACK : hi * PACK].bitcast(I32),
+                in_=y_codes[g][:, lo:hi].bitcast(I32),
+            )
+
+        def store_scales(g):
+            for quad in range(4):
+                queue = nc.sync if g < GROUPS - 1 or quad % 2 == 0 else nc.scalar
+                queue.dma_start(
+                    out=out_2[g, 4 * quad : 4 * quad + 4, :].bitcast(I32),
+                    in_=y_scales[g][32 * quad : 32 * quad + 4, :].bitcast(I32),
+                )
+
+        def quantize_y(u):
+            g, j, cnt = units[u]
+            cols = slice(j * P, (j + cnt) * P)
+            nc.vector.quantize_mx(
+                out=y_codes[g][:, cols].bitcast(E4M3X4),
+                scales=y_scales[g][:, cols],
+                in_=y_turned[u % RING][:, : cnt * N_TILE],
+            )
+            if g == GROUPS - 1 and j + cnt == S_TILES - 2:
+                store_planes(g, 0, (S_TILES - 2) * P)
+            if j + cnt == S_TILES:
+                store_planes(g, (S_TILES - 2) * P if g == GROUPS - 1 else 0, S)
+                store_scales(g)
+
+        splits = [VECTOR_COLS_HEAD] * (PASSES - 1) + [VECTOR_COLS_LAST]
+        for c in range(PASSES):
+            interleave_scalar(c, splits[c])
+        interleave_vector(0, splits[0])
+        quantize_a(0)
+        interleave_vector(1, splits[1])
+        for c in range(2, PASSES):
+            interleave_vector(c, splits[c])
+            quantize_a(c - 1)
+        quantize_a(PASSES - 1)
+        for w in range(WARM):
+            nc.tensor.matmul(out=acc[ACC_BANKS - 1][:], lhsT=ones[:], rhs=a_raw[PASSES - 2][:, 0, :], start=True, stop=True)
+        product(0)
+        spread_weight(0)
+
+        last = len(units) - 1
+        for i in range(len(units) + 3):
+            c = i + PASSES
+            opens_group = 0 < i + 1 <= last and units[i + 1][1] == 0
+            if i >= SQFIRST and i <= last:
+                subtract(i)
+                square(i)
+            if 0 <= i - 2 <= last - TAILV:
+                if i - 2 < GR0:
+                    round_y(i - 2, nc.scalar.copy)
+                else:
+                    round_y(i - 2, nc.scalar.copy, slice(0, 1))
+                    round_y(i - 2, gpsimd_copy, slice(1, 2))
+            if i + 1 <= last - LAST_EARLY:
+                product(i + 1, range(PASSES - 1) if opens_group else range(PASSES))
+            if LAST_EARLY and i + 2 == last:
+                product(last)
+            if 0 <= i - 2 <= last:
+                turn_y(i - 2)
+            if opens_group:
+                spread_weight(units[i + 1][0])
+            if i <= last and i < SQFIRST:
+                subtract(i)
+            if i == 0:
+                interleave_scalar(c, VECTOR_COLS_LOOP)
+                interleave_vector(c, VECTOR_COLS_LOOP)
+            elif c < PIECES and LOOP_V:
+                interleave_vector(c, LOOP_V)
+            if i <= last and i < SQFIRST:
+                square(i)
+            if 0 <= i - 3 <= last and not (QLATE and i >= last):
+                quantize_y(i - 3)
+            if c < PIECES:
+                quantize_a(c)
+            if opens_group:
+                product(i + 1, range(PASSES - 1, PASSES))
+            if c + 1 < PIECES:
+                lo = N_TILE - (GPSIMD_COLS if i > 0 else G_FIRST)
+                interleave_gpsimd(c + 1, lo)
+                interleave_scalar(c + 1, LOOP_V, lo)
+            if 0 <= i - 2 <= last:
+                copy_turned(i - 2)
+            if 0 <= i - 1 <= last:
+                weigh(i - 1)
+            if 0 <= i - 3 <= last and QLATE and i >= last:
+                quantize_y(i - 3)
+            if 0 <= i - 1 <= last:
+                if i - 1 > last - TAILV:
+                    round_y(i - 1, nc.vector.tensor_copy)

@@ -32,17 +32,14 @@ RING = 3
 VECTOR_COLS_HEAD = 256
 VECTOR_COLS_LOOP = 288
 VECTOR_COLS_LAST = 336
-GPSIMD_COLS = 384
-LOOP_V = 0
+GPSIMD_COLS = 336
+LOOP_V = 48
 G_FIRST = 208
 GR0 = 7
-QLATE = 1
-SQFIRST = 20
-LAST_EARLY = 0
 WARM = 5
-A_RING = 3
-PEORDER = 0
-TAILV = 2
+TURNED_RING = 5
+LORD = 0
+TORD = 0
 
 
 def tile_grasp_wrench_residual_k2_kernel(
@@ -64,7 +61,7 @@ def tile_grasp_wrench_residual_k2_kernel(
         def banks(name, count, shape):
             return [ps.tile(shape, F32, name="%s%d" % (name, i)) for i in range(count)]
 
-        f_scales = sb.tile([P, PASSES, S], U8, name="f_scales", align_bytes=64)
+        f_scales = tiles(sb, "f_scales", 2, [P, PASSES, S // 2], U8)
         f_words = tiles(sb, "f_words", S // F_CHUNK, [P, PASSES, F_CHUNK], U32)
         a_raw = tiles(sb, "a_raw", PIECES, [P, PACK, N_TILE], BF16)
         a_grouped = tiles(sb, "a_grouped", PASSES, [P, N_TILE * PACK], BF16)
@@ -74,7 +71,7 @@ def tile_grasp_wrench_residual_k2_kernel(
         y_sb = [sb.tile([P, cnt * N_TILE], F32, name="y%d" % i, align_bytes=64) for i, (g, j, cnt) in enumerate(units)]
         r_sb = tiles(sb, "r", RING, [P, 2 * N_TILE], F32)
         y_half = tiles(sb, "y_half", RING, [P, 2 * N_TILE], BF16)
-        y_turned = tiles(sb, "y_turned", RING, [P, 2 * N_TILE], BF16)
+        y_turned = tiles(sb, "y_turned", TURNED_RING, [P, 2 * N_TILE], BF16)
         y_codes = tiles(sb, "y_codes", GROUPS, [P, S], U32)
         y_scales = tiles(sb, "y_scales", GROUPS, [P, S], U8)
         weight_row = sb.tile([P, N], BF16, name="weight_row", align_bytes=64)
@@ -99,27 +96,33 @@ def tile_grasp_wrench_residual_k2_kernel(
             rows = wrench[j * P : (j + cnt) * P, g * N_TILE : (g + 1) * N_TILE]
             nc.sync.dma_start(out=wrench_sb[u][:], in_=rows.rearrange("(j p) n -> p j n", p=P))
 
-        nc.vector.memset(f_scales[:].rearrange("p k s -> p (k s)").bitcast(I32), 0)
+        def load_f_scales(half):
+            src = force_scales[:, :, half * (S // 2) : (half + 1) * (S // 2)].rearrange("k q s -> q k s")
+            for r in range(4):
+                nc.sync.dma_start(out=f_scales[half][r:P:32, :, :].bitcast(I32), in_=src[r:16:4].bitcast(I32))
+
+        for half in range(2):
+            nc.vector.memset(f_scales[half][:].rearrange("p k s -> p (k s)").bitcast(I32), 0)
         nc.vector.memset(weight_row[:].bitcast(I32), 0)
         nc.vector.memset(ones_src[:], 1.0)
         make_identity(nc, ident[:])
 
         for c in range(PASSES):
             load_a(c)
-        for quad in range(4):
-            nc.sync.dma_start(
-                out=f_scales[32 * quad : 32 * quad + 4, :, :].bitcast(I32),
-                in_=force_scales[:, 4 * quad : 4 * quad + 4, :].rearrange("k r s -> r k s").bitcast(I32),
-            )
+        load_f_scales(0)
         nc.scalar.activation(out=ones[:], in_=ones_src[:], func=ACT.Square)
         load_f(0)
         load_wrench(0)
         nc.sync.dma_start(out=weight_row[0:1, :], in_=weight.rearrange("(o n) -> o n", o=1))
-        for u in range(1, len(units)):
+        if LORD == 0:
+            load_f(1); load_a(4); load_wrench(1); load_f_scales(1); load_a(5)
+        if LORD == 1:
+            load_a(4); load_f(1); load_wrench(1); load_a(5); load_f_scales(1)
+        if LORD == 2:
+            load_f(1); load_a(4); load_wrench(1); load_a(5); load_f_scales(1)
+        for u in range(2, len(units)):
             if u < S // F_CHUNK:
                 load_f(u)
-            if u == 1:
-                load_a(PASSES)
             load_wrench(u)
             if u + PASSES < PIECES:
                 load_a(u + PASSES)
@@ -150,10 +153,11 @@ def tile_grasp_wrench_residual_k2_kernel(
         def mx_pass(u, jj, k):
             g, j, cnt = units[u]
             q, off = divmod((j + jj) * P, F_CHUNK)
+            half, s0 = divmod((j + jj) * P, S // 2)
             nc.tensor.matmul_mx(
                 out=acc[(first_tile[u] + jj) % ACC_BANKS][:],
                 lhsT=f_words[q][:, k, off : off + P].bitcast(E5M2X4),
-                lhsT_scale=f_scales[:, k, (j + jj) * P : (j + jj + 1) * P],
+                lhsT_scale=f_scales[half][:, k, s0 : s0 + P],
                 rhs=a_codes[g * PASSES + k][:].bitcast(E4M3X4),
                 rhs_scale=a_scales[g * PASSES + k][:],
                 start=(k == 0),
@@ -216,7 +220,7 @@ def tile_grasp_wrench_residual_k2_kernel(
         def copy_turned(u):
             cnt = units[u][2]
             nc.scalar.copy(
-                out=y_turned[u % RING][:, : cnt * N_TILE].bitcast(F32).rearrange("p (m h) -> p m h", h=2),
+                out=y_turned[u % TURNED_RING][:, : cnt * N_TILE].bitcast(F32).rearrange("p (m h) -> p m h", h=2),
                 in_=turn[u % TURN_BANKS][:, : 2 * cnt * P].rearrange("p (h m) -> p m h", h=2),
             )
 
@@ -227,12 +231,9 @@ def tile_grasp_wrench_residual_k2_kernel(
             )
 
         def store_scales(g):
-            for quad in range(4):
-                queue = nc.sync if g < GROUPS - 1 or quad % 2 == 0 else nc.scalar
-                queue.dma_start(
-                    out=out_2[g, 4 * quad : 4 * quad + 4, :].bitcast(I32),
-                    in_=y_scales[g][32 * quad : 32 * quad + 4, :].bitcast(I32),
-                )
+            for r in range(4):
+                queue = nc.sync if g < GROUPS - 1 or r % 2 == 0 else nc.scalar
+                queue.dma_start(out=out_2[g, r:16:4, :].bitcast(I32), in_=y_scales[g][r:P:32, :].bitcast(I32))
 
         def quantize_y(u):
             g, j, cnt = units[u]
@@ -240,7 +241,7 @@ def tile_grasp_wrench_residual_k2_kernel(
             nc.vector.quantize_mx(
                 out=y_codes[g][:, cols].bitcast(E4M3X4),
                 scales=y_scales[g][:, cols],
-                in_=y_turned[u % RING][:, : cnt * N_TILE],
+                in_=y_turned[u % TURNED_RING][:, : cnt * N_TILE],
             )
             if g == GROUPS - 1 and j + cnt == S_TILES - 2:
                 store_planes(g, 0, (S_TILES - 2) * P)
@@ -263,52 +264,95 @@ def tile_grasp_wrench_residual_k2_kernel(
         product(0)
         spread_weight(0)
 
+        def round_shared(u):
+            round_y(u, nc.scalar.copy, slice(0, 1))
+            round_y(u, gpsimd_copy, slice(1, 2))
+
         last = len(units) - 1
-        for i in range(len(units) + 3):
+        interleave_scalar(PASSES, VECTOR_COLS_LOOP)
+        for i in range(last - 1):
             c = i + PASSES
-            opens_group = 0 < i + 1 <= last and units[i + 1][1] == 0
-            if i >= SQFIRST and i <= last:
-                subtract(i)
-                square(i)
-            if 0 <= i - 2 <= last - TAILV:
+            opens_group = units[i + 1][1] == 0
+            if i >= 2:
                 if i - 2 < GR0:
                     round_y(i - 2, nc.scalar.copy)
                 else:
-                    round_y(i - 2, nc.scalar.copy, slice(0, 1))
-                    round_y(i - 2, gpsimd_copy, slice(1, 2))
-            if i + 1 <= last - LAST_EARLY:
-                product(i + 1, range(PASSES - 1) if opens_group else range(PASSES))
-            if LAST_EARLY and i + 2 == last:
-                product(last)
-            if 0 <= i - 2 <= last:
+                    round_shared(i - 2)
+            product(i + 1, range(PASSES - 1) if opens_group else range(PASSES))
+            if i >= 2:
                 turn_y(i - 2)
             if opens_group:
                 spread_weight(units[i + 1][0])
-            if i <= last and i < SQFIRST:
-                subtract(i)
+            subtract(i)
             if i == 0:
-                interleave_scalar(c, VECTOR_COLS_LOOP)
                 interleave_vector(c, VECTOR_COLS_LOOP)
-            elif c < PIECES and LOOP_V:
-                interleave_vector(c, LOOP_V)
-            if i <= last and i < SQFIRST:
-                square(i)
-            if 0 <= i - 3 <= last and not (QLATE and i >= last):
-                quantize_y(i - 3)
+            square(i)
             if c < PIECES:
                 quantize_a(c)
             if opens_group:
                 product(i + 1, range(PASSES - 1, PASSES))
+            if i >= 3:
+                quantize_y(i - 3)
             if c + 1 < PIECES:
                 lo = N_TILE - (GPSIMD_COLS if i > 0 else G_FIRST)
+                interleave_vector(c + 1, LOOP_V)
                 interleave_gpsimd(c + 1, lo)
                 interleave_scalar(c + 1, LOOP_V, lo)
-            if 0 <= i - 2 <= last:
+            if i >= 2:
                 copy_turned(i - 2)
-            if 0 <= i - 1 <= last:
+            if i >= 1:
                 weigh(i - 1)
-            if 0 <= i - 3 <= last and QLATE and i >= last:
-                quantize_y(i - 3)
-            if 0 <= i - 1 <= last:
-                if i - 1 > last - TAILV:
-                    round_y(i - 1, nc.vector.tensor_copy)
+
+        a, b, z = last - 2, last - 1, last
+        if TORD == 0:
+            round_shared(a - 1)
+            product(z)
+            turn_y(a - 1)
+            subtract(b)
+            square(b)
+            weigh(a)
+            copy_turned(a - 1)
+            subtract(z)
+            square(z)
+            round_shared(a)
+            turn_y(a)
+            weigh(b)
+            weigh(z)
+            round_y(b, nc.scalar.copy)
+            quantize_y(a - 2)
+            round_y(z, nc.vector.tensor_copy)
+            copy_turned(a)
+            turn_y(b)
+            turn_y(z)
+            quantize_y(a - 1)
+            copy_turned(b)
+            copy_turned(z)
+            quantize_y(a)
+            quantize_y(b)
+            quantize_y(z)
+        if TORD == 1:
+            round_shared(a - 1)
+            product(z)
+            turn_y(a - 1)
+            subtract(b)
+            square(b)
+            weigh(a)
+            copy_turned(a - 1)
+            subtract(z)
+            square(z)
+            round_shared(a)
+            turn_y(a)
+            weigh(b)
+            round_y(b, gpsimd_copy)
+            weigh(z)
+            copy_turned(a)
+            round_y(z, nc.scalar.copy)
+            quantize_y(a - 2)
+            quantize_y(a - 1)
+            turn_y(b)
+            turn_y(z)
+            quantize_y(a)
+            copy_turned(b)
+            copy_turned(z)
+            quantize_y(b)
+            quantize_y(z)

@@ -22,24 +22,25 @@ K_PASS = P * PACK
 PASSES = K // K_PASS
 N_TILE = 512
 GROUPS = N // N_TILE
-S_TILES = S // P
-F_CHUNK = 2 * P
 PIECES = GROUPS * PASSES
-HEAD_PIECES = PASSES + 1
+CASE_TILES = S // P
+PAIR = 2
+F_CHUNK = PAIR * P
+S_HALF = S // 2
+SCALE_ROWS = 4
+QUADRANT = 32
+RUN = 4
+
 ACC_BANKS = 4
 TURN_BANKS = 2
+WEIGHT_BANKS = 2
 RING = 3
-VECTOR_COLS_HEAD = 256
-VECTOR_COLS_LOOP = 288
-VECTOR_COLS_LAST = 336
-GPSIMD_COLS = 336
-LOOP_V = 48
-G_FIRST = 208
-GR0 = 7
-WARM = 5
 TURNED_RING = 5
-LORD = 0
-TORD = 0
+
+EVEN_SHARE = N_TILE // 2
+GPSIMD_SHARE = 320
+GPSIMD_FIRST_SHARE = 208
+VECTOR_SHARE = 64
 
 
 def tile_grasp_wrench_residual_k2_kernel(
@@ -47,40 +48,43 @@ def tile_grasp_wrench_residual_k2_kernel(
 ):
     nc = tc.nc
 
-    units = [(g, j, 2) for g in range(GROUPS) for j in range(0, S_TILES, 2)]
-    units = units[:-1] + [(GROUPS - 1, S_TILES - 2, 1), (GROUPS - 1, S_TILES - 1, 1)]
+    units = [(g, j, PAIR) for g in range(GROUPS) for j in range(0, CASE_TILES, PAIR)]
+    units = units[:-1] + [(GROUPS - 1, CASE_TILES - 2, 1), (GROUPS - 1, CASE_TILES - 1, 1)]
+    last = len(units) - 1
+    first_tile = [sum(count for g, j, count in units[:u]) for u in range(len(units))]
 
     with ExitStack() as ctx:
         sb = ctx.enter_context(tc.tile_pool(name="sb", bufs=1))
         ps = ctx.enter_context(tc.psum_pool(name="ps", bufs=1))
         ctx.enter_context(tc.manual_schedule())
 
-        def tiles(pool, name, count, shape, dtype):
-            return [pool.tile(shape, dtype, name="%s%d" % (name, i), align_bytes=64) for i in range(count)]
+        def tiles(name, shapes, dtype):
+            return [sb.tile(shape, dtype, name="%s%d" % (name, i), align_bytes=64) for i, shape in enumerate(shapes)]
 
-        def banks(name, count, shape):
-            return [ps.tile(shape, F32, name="%s%d" % (name, i)) for i in range(count)]
+        def banks(name, count):
+            return [ps.tile([P, N_TILE], F32, name="%s%d" % (name, i)) for i in range(count)]
 
-        f_scales = tiles(sb, "f_scales", 2, [P, PASSES, S // 2], U8)
-        f_words = tiles(sb, "f_words", S // F_CHUNK, [P, PASSES, F_CHUNK], U32)
-        a_raw = tiles(sb, "a_raw", PIECES, [P, PACK, N_TILE], BF16)
-        a_grouped = tiles(sb, "a_grouped", PASSES, [P, N_TILE * PACK], BF16)
-        a_codes = tiles(sb, "a_codes", PIECES, [P, N_TILE], U32)
-        a_scales = tiles(sb, "a_scales", PIECES, [P, N_TILE], U8)
-        wrench_sb = [sb.tile([P, cnt, N_TILE], BF16, name="wrench%d" % i, align_bytes=64) for i, (g, j, cnt) in enumerate(units)]
-        y_sb = [sb.tile([P, cnt * N_TILE], F32, name="y%d" % i, align_bytes=64) for i, (g, j, cnt) in enumerate(units)]
-        r_sb = tiles(sb, "r", RING, [P, 2 * N_TILE], F32)
-        y_half = tiles(sb, "y_half", RING, [P, 2 * N_TILE], BF16)
-        y_turned = tiles(sb, "y_turned", TURNED_RING, [P, 2 * N_TILE], BF16)
-        y_codes = tiles(sb, "y_codes", GROUPS, [P, S], U32)
-        y_scales = tiles(sb, "y_scales", GROUPS, [P, S], U8)
+        f_scales = tiles("f_scales", [[P, PASSES, S_HALF]] * (S // S_HALF), U8)
+        f_words = tiles("f_words", [[P, PASSES, F_CHUNK]] * (S // F_CHUNK), U32)
+        a_raw = tiles("a_raw", [[P, PACK, N_TILE]] * PIECES, BF16)
+        a_grouped = tiles("a_grouped", [[P, N_TILE * PACK]] * PASSES, BF16)
+        a_codes = tiles("a_codes", [[P, N_TILE]] * PIECES, U32)
+        a_scales = tiles("a_scales", [[P, N_TILE]] * PIECES, U8)
+        wrench_sb = tiles("wrench", [[P, count, N_TILE] for g, j, count in units], BF16)
+        y_sb = tiles("y", [[P, count * N_TILE] for g, j, count in units], F32)
+        r_sb = tiles("r", [[P, PAIR * N_TILE]] * RING, F32)
+        y_rounded = tiles("y_rounded", [[P, PAIR * N_TILE]] * RING, BF16)
+        y_turned = tiles("y_turned", [[P, PAIR * N_TILE]] * TURNED_RING, BF16)
+        y_codes = tiles("y_codes", [[P, S]] * GROUPS, U32)
+        y_scales = tiles("y_scales", [[P, S]] * GROUPS, U8)
         weight_row = sb.tile([P, N], BF16, name="weight_row", align_bytes=64)
         ones_src = sb.tile([P, P], BF16, name="ones_src", align_bytes=64)
         ones = sb.tile([P, P], BF16, name="ones", align_bytes=64)
         ident = sb.tile([P, P], F32, name="ident", align_bytes=64)
-        acc = banks("acc", ACC_BANKS, [P, N_TILE])
-        turn = banks("turn", TURN_BANKS, [P, N_TILE])
-        weight_bank = banks("weight_bank", 2, [P, N_TILE])
+        acc = banks("acc", ACC_BANKS)
+        turn = banks("turn", TURN_BANKS)
+        weight_bank = banks("weight_bank", WEIGHT_BANKS)
+
 
         def load_a(c):
             g, k = divmod(c, PASSES)
@@ -88,271 +92,264 @@ def tile_grasp_wrench_residual_k2_kernel(
             nc.sync.dma_start(out=a_raw[c][:], in_=rows.rearrange("(p t) n -> p t n", t=PACK))
 
         def load_f(q):
-            src = force_words.rearrange("k p s t -> p k (s t)")[:, :, q * F_CHUNK * PACK : (q + 1) * F_CHUNK * PACK]
-            nc.sync.dma_start(out=f_words[q][:].bitcast(I32), in_=src.bitcast(I32))
-
-        def load_wrench(u):
-            g, j, cnt = units[u]
-            rows = wrench[j * P : (j + cnt) * P, g * N_TILE : (g + 1) * N_TILE]
-            nc.sync.dma_start(out=wrench_sb[u][:], in_=rows.rearrange("(j p) n -> p j n", p=P))
+            cases = force_words.rearrange("k p s t -> p k (s t)")[:, :, q * F_CHUNK * PACK : (q + 1) * F_CHUNK * PACK]
+            nc.sync.dma_start(out=f_words[q][:].bitcast(I32), in_=cases.bitcast(I32))
 
         def load_f_scales(half):
-            src = force_scales[:, :, half * (S // 2) : (half + 1) * (S // 2)].rearrange("k q s -> q k s")
-            for r in range(4):
-                nc.sync.dma_start(out=f_scales[half][r:P:32, :, :].bitcast(I32), in_=src[r:16:4].bitcast(I32))
+            rows = force_scales[:, :, half * S_HALF : (half + 1) * S_HALF].rearrange("k q s -> q k s")
+            for r in range(SCALE_ROWS):
+                nc.sync.dma_start(
+                    out=f_scales[half][r:P:QUADRANT, :, :].bitcast(I32), in_=rows[r : 4 * SCALE_ROWS : SCALE_ROWS].bitcast(I32)
+                )
 
-        for half in range(2):
-            nc.vector.memset(f_scales[half][:].rearrange("p k s -> p (k s)").bitcast(I32), 0)
+        def load_wrench(u):
+            g, j, count = units[u]
+            rows = wrench[j * P : (j + count) * P, g * N_TILE : (g + 1) * N_TILE]
+            nc.sync.dma_start(out=wrench_sb[u][:], in_=rows.rearrange("(j p) n -> p j n", p=P))
+
+        for tile in f_scales:
+            nc.vector.memset(tile[:].rearrange("p k s -> p (k s)").bitcast(I32), 0)
         nc.vector.memset(weight_row[:].bitcast(I32), 0)
         nc.vector.memset(ones_src[:], 1.0)
         make_identity(nc, ident[:])
+        nc.scalar.activation(out=ones[:], in_=ones_src[:], func=ACT.Square)
 
         for c in range(PASSES):
             load_a(c)
         load_f_scales(0)
-        nc.scalar.activation(out=ones[:], in_=ones_src[:], func=ACT.Square)
         load_f(0)
         load_wrench(0)
         nc.sync.dma_start(out=weight_row[0:1, :], in_=weight.rearrange("(o n) -> o n", o=1))
-        if LORD == 0:
-            load_f(1); load_a(4); load_wrench(1); load_f_scales(1); load_a(5)
-        if LORD == 1:
-            load_a(4); load_f(1); load_wrench(1); load_a(5); load_f_scales(1)
-        if LORD == 2:
-            load_f(1); load_a(4); load_wrench(1); load_a(5); load_f_scales(1)
-        for u in range(2, len(units)):
-            if u < S // F_CHUNK:
+        load_a(PASSES)
+        for u in range(1, len(units)):
+            if u * F_CHUNK == S_HALF:
+                load_f_scales(1)
+            if u < len(f_words):
                 load_f(u)
             load_wrench(u)
             if u + PASSES < PIECES:
                 load_a(u + PASSES)
 
+
+        def grouped(c):
+            return a_grouped[min(c, PASSES - 1)]
+
         def interleave(engine_copy, c, lo, hi):
-            dst = a_grouped[min(c, PASSES - 1)][:, lo * PACK : hi * PACK].rearrange("p (c i t) -> p c t i", i=4, t=PACK)
-            src = a_raw[c][:, :, lo:hi].rearrange("p t (c i) -> p c t i", i=4)
-            engine_copy(out=dst, in_=src)
-
-        def interleave_vector(c, split):
-            interleave(nc.vector.tensor_copy, c, 0, split)
-
-        def interleave_scalar(c, split, end=N_TILE):
-            interleave(nc.scalar.copy, c, split, end)
-
-        def interleave_gpsimd(c, lo):
-            nc.gpsimd.tensor_scalar(
-                out=a_grouped[min(c, PASSES - 1)][:, lo * PACK :].rearrange("p (c t) -> p c t", t=PACK),
-                in0=a_raw[c][:, :, lo:].rearrange("p t c -> p c t"),
-                scalar1=1.0, scalar2=0.0, op0=ALU.mult, op1=ALU.add,
+            engine_copy(
+                out=grouped(c)[:, lo * PACK : hi * PACK].rearrange("p (c i t) -> p c t i", i=RUN, t=PACK),
+                in_=a_raw[c][:, :, lo:hi].rearrange("p t (c i) -> p c t i", i=RUN),
             )
 
-        def quantize_a(c):
-            nc.vector.quantize_mx(out=a_codes[c][:].bitcast(E4M3X4), scales=a_scales[c][:], in_=a_grouped[min(c, PASSES - 1)][:])
+        def gpsimd_copy(out, in_):
+            nc.gpsimd.tensor_scalar(out=out, in0=in_, scalar1=1.0, scalar2=0.0, op0=ALU.mult, op1=ALU.add)
 
-        first_tile = [sum(cnt for g, j, cnt in units[:u]) for u in range(len(units))]
+        def interleave_gpsimd(c, lo):
+            gpsimd_copy(
+                out=grouped(c)[:, lo * PACK :].rearrange("p (c t) -> p c t", t=PACK),
+                in_=a_raw[c][:, :, lo:].rearrange("p t c -> p c t"),
+            )
+
+        def vector_share(c):
+            return VECTOR_SHARE if c >= PIECES - PASSES else 0
+
+        def quantize_a(c):
+            nc.vector.quantize_mx(out=a_codes[c][:].bitcast(E4M3X4), scales=a_scales[c][:], in_=grouped(c)[:])
+
+
+        def acc_bank(u, jj):
+            return acc[(first_tile[u] + jj) % ACC_BANKS]
 
         def mx_pass(u, jj, k):
-            g, j, cnt = units[u]
-            q, off = divmod((j + jj) * P, F_CHUNK)
-            half, s0 = divmod((j + jj) * P, S // 2)
+            g, j, count = units[u]
+            q, in_chunk = divmod((j + jj) * P, F_CHUNK)
+            half, in_half = divmod((j + jj) * P, S_HALF)
             nc.tensor.matmul_mx(
-                out=acc[(first_tile[u] + jj) % ACC_BANKS][:],
-                lhsT=f_words[q][:, k, off : off + P].bitcast(E5M2X4),
-                lhsT_scale=f_scales[half][:, k, s0 : s0 + P],
+                out=acc_bank(u, jj)[:],
+                lhsT=f_words[q][:, k, in_chunk : in_chunk + P].bitcast(E5M2X4),
+                lhsT_scale=f_scales[half][:, k, in_half : in_half + P],
                 rhs=a_codes[g * PASSES + k][:].bitcast(E4M3X4),
                 rhs_scale=a_scales[g * PASSES + k][:],
                 start=(k == 0),
                 stop=(k == PASSES - 1),
             )
 
-        def product(u, passes=range(PASSES)):
-            if u > 0 and units[u][1] == 0:
-                for k in passes:
-                    for jj in range(units[u][2]):
-                        mx_pass(u, jj, k)
-            else:
+        def product(u):
+            for jj in range(units[u][2]):
+                for k in range(PASSES):
+                    mx_pass(u, jj, k)
+
+        def product_passes(u, passes):
+            for k in passes:
                 for jj in range(units[u][2]):
-                    for k in passes:
-                        mx_pass(u, jj, k)
+                    mx_pass(u, jj, k)
 
         def spread_weight(g):
             nc.tensor.matmul(
-                out=weight_bank[g % 2][:], lhsT=ones[:], rhs=weight_row[:, g * N_TILE : (g + 1) * N_TILE], start=True, stop=True
+                out=weight_bank[g % WEIGHT_BANKS][:],
+                lhsT=ones[:],
+                rhs=weight_row[:, g * N_TILE : (g + 1) * N_TILE],
+                start=True,
+                stop=True,
             )
 
         def subtract(u):
             for jj in range(units[u][2]):
                 nc.vector.tensor_tensor(
                     out=r_sb[u % RING][:, jj * N_TILE : (jj + 1) * N_TILE],
-                    in0=acc[(first_tile[u] + jj) % ACC_BANKS][:],
+                    in0=acc_bank(u, jj)[:],
                     in1=wrench_sb[u][:, jj, :],
                     op=ALU.subtract,
                 )
 
         def square(u):
-            width = units[u][2] * N_TILE
-            nc.scalar.activation(out=y_sb[u][:], in_=r_sb[u % RING][:, :width], func=ACT.Square)
+            nc.scalar.activation(out=y_sb[u][:], in_=r_sb[u % RING][:, : units[u][2] * N_TILE], func=ACT.Square)
 
         def weigh(u):
-            g, j, cnt = units[u]
-            y3 = y_sb[u][:].rearrange("p (j n) -> p j n", j=cnt)
+            g, j, count = units[u]
+            y_tiles = y_sb[u][:].rearrange("p (j n) -> p j n", j=count)
             nc.vector.tensor_tensor(
-                out=y3, in0=y3, in1=weight_bank[g % 2][:].unsqueeze(1).to_broadcast([P, cnt, N_TILE]), op=ALU.mult
+                out=y_tiles,
+                in0=y_tiles,
+                in1=weight_bank[g % WEIGHT_BANKS][:].unsqueeze(1).to_broadcast([P, count, N_TILE]),
+                op=ALU.mult,
             )
-            rows = out_0[j * P : (j + cnt) * P, g * N_TILE : (g + 1) * N_TILE]
-            nc.sync.dma_start(out=rows.rearrange("(j p) n -> p j n", p=P), in_=y3)
-
-        def gpsimd_copy(out, in_):
-            nc.gpsimd.tensor_scalar(out=out, in0=in_, scalar1=1.0, scalar2=0.0, op0=ALU.mult, op1=ALU.add)
+            rows = out_0[j * P : (j + count) * P, g * N_TILE : (g + 1) * N_TILE]
+            nc.sync.dma_start(out=rows.rearrange("(j p) n -> p j n", p=P), in_=y_tiles)
 
         def round_y(u, engine_copy, halves=slice(0, 2)):
             width = units[u][2] * N_TILE
             engine_copy(
-                out=y_half[u % RING][:, :width].rearrange("p (h m e) -> p h m e", h=2, e=2)[:, halves],
+                out=y_rounded[u % RING][:, :width].rearrange("p (h m e) -> p h m e", h=2, e=2)[:, halves],
                 in_=y_sb[u][:].rearrange("p (m h e) -> p h m e", h=2, e=2)[:, halves],
             )
-
-        def turn_y(u):
-            cnt = units[u][2]
-            words = y_half[u % RING][:, : cnt * N_TILE].bitcast(F32)
-            for b in range(2 * cnt):
-                nc.tensor.transpose(turn[u % TURN_BANKS][:, b * P : (b + 1) * P], words[:, b * P : (b + 1) * P], ident[:])
-
-        def copy_turned(u):
-            cnt = units[u][2]
-            nc.scalar.copy(
-                out=y_turned[u % TURNED_RING][:, : cnt * N_TILE].bitcast(F32).rearrange("p (m h) -> p m h", h=2),
-                in_=turn[u % TURN_BANKS][:, : 2 * cnt * P].rearrange("p (h m) -> p m h", h=2),
-            )
-
-        def store_planes(g, lo, hi):
-            nc.sync.dma_start(
-                out=out_1[g].rearrange("p m t -> p (m t)")[:, lo * PACK : hi * PACK].bitcast(I32),
-                in_=y_codes[g][:, lo:hi].bitcast(I32),
-            )
-
-        def store_scales(g):
-            for r in range(4):
-                queue = nc.sync if g < GROUPS - 1 or r % 2 == 0 else nc.scalar
-                queue.dma_start(out=out_2[g, r:16:4, :].bitcast(I32), in_=y_scales[g][r:P:32, :].bitcast(I32))
-
-        def quantize_y(u):
-            g, j, cnt = units[u]
-            cols = slice(j * P, (j + cnt) * P)
-            nc.vector.quantize_mx(
-                out=y_codes[g][:, cols].bitcast(E4M3X4),
-                scales=y_scales[g][:, cols],
-                in_=y_turned[u % TURNED_RING][:, : cnt * N_TILE],
-            )
-            if g == GROUPS - 1 and j + cnt == S_TILES - 2:
-                store_planes(g, 0, (S_TILES - 2) * P)
-            if j + cnt == S_TILES:
-                store_planes(g, (S_TILES - 2) * P if g == GROUPS - 1 else 0, S)
-                store_scales(g)
-
-        splits = [VECTOR_COLS_HEAD] * (PASSES - 1) + [VECTOR_COLS_LAST]
-        for c in range(PASSES):
-            interleave_scalar(c, splits[c])
-        interleave_vector(0, splits[0])
-        quantize_a(0)
-        interleave_vector(1, splits[1])
-        for c in range(2, PASSES):
-            interleave_vector(c, splits[c])
-            quantize_a(c - 1)
-        quantize_a(PASSES - 1)
-        for w in range(WARM):
-            nc.tensor.matmul(out=acc[ACC_BANKS - 1][:], lhsT=ones[:], rhs=a_raw[PASSES - 2][:, 0, :], start=True, stop=True)
-        product(0)
-        spread_weight(0)
 
         def round_shared(u):
             round_y(u, nc.scalar.copy, slice(0, 1))
             round_y(u, gpsimd_copy, slice(1, 2))
 
-        last = len(units) - 1
-        interleave_scalar(PASSES, VECTOR_COLS_LOOP)
+        def turn_bank(u):
+            return acc[last - u] if u >= last - 1 else turn[u % TURN_BANKS]
+
+        def turn_y(u):
+            count = units[u][2]
+            words = y_rounded[u % RING][:, : count * N_TILE].bitcast(F32)
+            for b in range(2 * count):
+                nc.tensor.transpose(turn_bank(u)[:, b * P : (b + 1) * P], words[:, b * P : (b + 1) * P], ident[:])
+
+        def copy_turned(u):
+            count = units[u][2]
+            nc.scalar.copy(
+                out=y_turned[u % TURNED_RING][:, : count * N_TILE].bitcast(F32).rearrange("p (s h) -> p s h", h=2),
+                in_=turn_bank(u)[:, : 2 * count * P].rearrange("p (h s) -> p s h", h=2),
+            )
+
+        def quantize_y_tiles(u, lo, hi):
+            g, j, count = units[u]
+            cases = slice((j + lo) * P, (j + hi) * P)
+            nc.vector.quantize_mx(
+                out=y_codes[g][:, cases].bitcast(E4M3X4),
+                scales=y_scales[g][:, cases],
+                in_=y_turned[u % TURNED_RING][:, lo * N_TILE : hi * N_TILE],
+            )
+
+        def quantize_y(u):
+            quantize_y_tiles(u, 0, units[u][2])
+
+        def store_words(g, lo, hi):
+            nc.sync.dma_start(
+                out=out_1[g].rearrange("p s t -> p (s t)")[:, lo * PACK : hi * PACK].bitcast(I32),
+                in_=y_codes[g][:, lo:hi].bitcast(I32),
+            )
+
+        def store_scales(g, queues):
+            for r in range(SCALE_ROWS):
+                queues[r % len(queues)].dma_start(
+                    out=out_2[g, r : 4 * SCALE_ROWS : SCALE_ROWS, :].bitcast(I32),
+                    in_=y_scales[g][r:P:QUADRANT, :].bitcast(I32),
+                )
+
+        for c in range(PASSES):
+            interleave(nc.scalar.copy, c, EVEN_SHARE, N_TILE)
+        interleave(nc.vector.tensor_copy, 0, 0, EVEN_SHARE)
+        quantize_a(0)
+        interleave(nc.vector.tensor_copy, 1, 0, EVEN_SHARE)
+        for c in range(2, PASSES):
+            interleave(nc.vector.tensor_copy, c, 0, EVEN_SHARE)
+            quantize_a(c - 1)
+        quantize_a(PASSES - 1)
+        product(0)
+        spread_weight(0)
+        interleave(nc.scalar.copy, PASSES, EVEN_SHARE, N_TILE)
+
         for i in range(last - 1):
             c = i + PASSES
             opens_group = units[i + 1][1] == 0
             if i >= 2:
-                if i - 2 < GR0:
+                if c - 1 < PIECES:
                     round_y(i - 2, nc.scalar.copy)
                 else:
                     round_shared(i - 2)
-            product(i + 1, range(PASSES - 1) if opens_group else range(PASSES))
+            if opens_group:
+                product_passes(i + 1, range(PASSES - 1))
+            else:
+                product(i + 1)
             if i >= 2:
                 turn_y(i - 2)
             if opens_group:
                 spread_weight(units[i + 1][0])
             subtract(i)
             if i == 0:
-                interleave_vector(c, VECTOR_COLS_LOOP)
+                interleave(nc.vector.tensor_copy, c, 0, EVEN_SHARE)
+            shares_piece = c < PIECES and vector_share(c) > 0
+            if shares_piece:
+                interleave(nc.vector.tensor_copy, c, 0, vector_share(c))
             square(i)
+            if shares_piece:
+                quantize_y_tiles(i - 3, 0, 1)
             if c < PIECES:
                 quantize_a(c)
             if opens_group:
-                product(i + 1, range(PASSES - 1, PASSES))
+                product_passes(i + 1, [PASSES - 1])
             if i >= 3:
-                quantize_y(i - 3)
+                quantize_y_tiles(i - 3, 1 if shares_piece else 0, PAIR)
+                if units[i - 3][1] + PAIR == CASE_TILES:
+                    store_words(units[i - 3][0], 0, S)
+                    store_scales(units[i - 3][0], [nc.sync])
             if c + 1 < PIECES:
-                lo = N_TILE - (GPSIMD_COLS if i > 0 else G_FIRST)
-                interleave_vector(c + 1, LOOP_V)
-                interleave_gpsimd(c + 1, lo)
-                interleave_scalar(c + 1, LOOP_V, lo)
+                gpsimd_from = N_TILE - (GPSIMD_SHARE if i > 0 else GPSIMD_FIRST_SHARE)
+                interleave_gpsimd(c + 1, gpsimd_from)
+                interleave(nc.scalar.copy, c + 1, vector_share(c + 1), gpsimd_from)
             if i >= 2:
                 copy_turned(i - 2)
             if i >= 1:
                 weigh(i - 1)
 
-        a, b, z = last - 2, last - 1, last
-        if TORD == 0:
-            round_shared(a - 1)
-            product(z)
-            turn_y(a - 1)
-            subtract(b)
-            square(b)
-            weigh(a)
-            copy_turned(a - 1)
-            subtract(z)
-            square(z)
-            round_shared(a)
-            turn_y(a)
-            weigh(b)
-            weigh(z)
-            round_y(b, nc.scalar.copy)
-            quantize_y(a - 2)
-            round_y(z, nc.vector.tensor_copy)
-            copy_turned(a)
-            turn_y(b)
-            turn_y(z)
-            quantize_y(a - 1)
-            copy_turned(b)
-            copy_turned(z)
-            quantize_y(a)
-            quantize_y(b)
-            quantize_y(z)
-        if TORD == 1:
-            round_shared(a - 1)
-            product(z)
-            turn_y(a - 1)
-            subtract(b)
-            square(b)
-            weigh(a)
-            copy_turned(a - 1)
-            subtract(z)
-            square(z)
-            round_shared(a)
-            turn_y(a)
-            weigh(b)
-            round_y(b, gpsimd_copy)
-            weigh(z)
-            copy_turned(a)
-            round_y(z, nc.scalar.copy)
-            quantize_y(a - 2)
-            quantize_y(a - 1)
-            turn_y(b)
-            turn_y(z)
-            quantize_y(a)
-            copy_turned(b)
-            copy_turned(z)
-            quantize_y(b)
-            quantize_y(z)
+        pair, single, final = last - 2, last - 1, last
+        round_shared(pair - 1)
+        product(final)
+        turn_y(pair - 1)
+        subtract(single)
+        square(single)
+        weigh(pair)
+        round_shared(pair)
+        subtract(final)
+        square(final)
+        copy_turned(pair - 1)
+        turn_y(pair)
+        weigh(single)
+        round_y(single, nc.vector.tensor_copy)
+        weigh(final)
+        quantize_y(pair - 2)
+        round_y(final, nc.vector.tensor_copy)
+        for u in (single, final):
+            turn_y(u)
+        for u in (pair, single, final):
+            copy_turned(u)
+        quantize_y(pair - 1)
+        quantize_y(pair)
+        singles_from = units[single][1] * P
+        store_words(GROUPS - 1, 0, singles_from)
+        quantize_y(single)
+        quantize_y(final)
+        store_words(GROUPS - 1, singles_from, S)
+        store_scales(GROUPS - 1, [nc.scalar, nc.sync])

from contextlib import ExitStack

import concourse.mybir as mybir
from concourse.masks import make_identity

S, K, N = 1024, 2048, 1536
FLOPS = 2 * S * K * N

F32 = mybir.dt.float32
BF16 = mybir.dt.bfloat16
I32 = mybir.dt.int32
U32 = mybir.dt.uint32
U8 = mybir.dt.uint8
E4M3X4 = mybir.dt.float8_e4m3fn_x4
E5M2X4 = mybir.dt.float8_e5m2_x4
ALU = mybir.AluOpType
ACT = mybir.ActivationFunctionType

P = 128
PACK = 4
K_PASS = P * PACK
PASSES = K // K_PASS
N_TILE = 512
GROUPS = N // N_TILE
PIECES = GROUPS * PASSES
CASE_TILES = S // P
PAIR = 2
F_CHUNK = PAIR * P
S_HALF = S // 2
SCALE_ROWS = 4
QUADRANT = 32
RUN = 4

ACC_BANKS = 4
TURN_BANKS = 2
WEIGHT_BANKS = 2
RING = 3
TURNED_RING = 5

EVEN_SHARE = N_TILE // 2
GPSIMD_SHARE = 320
GPSIMD_FIRST_SHARE = 208
VECTOR_SHARE = 64


def tile_grasp_wrench_residual_k2_kernel(
    tc, force_words, force_scales, grasp_t, wrench, weight, out_0, out_1, out_2
):
    nc = tc.nc

    units = [(g, j, PAIR) for g in range(GROUPS) for j in range(0, CASE_TILES, PAIR)]
    units = units[:-1] + [(GROUPS - 1, CASE_TILES - 2, 1), (GROUPS - 1, CASE_TILES - 1, 1)]
    last = len(units) - 1
    first_tile = [sum(count for g, j, count in units[:u]) for u in range(len(units))]

    with ExitStack() as ctx:
        sb = ctx.enter_context(tc.tile_pool(name="sb", bufs=1))
        ps = ctx.enter_context(tc.psum_pool(name="ps", bufs=1))
        ctx.enter_context(tc.manual_schedule())

        def tiles(name, shapes, dtype):
            return [sb.tile(shape, dtype, name="%s%d" % (name, i), align_bytes=64) for i, shape in enumerate(shapes)]

        def banks(name, count):
            return [ps.tile([P, N_TILE], F32, name="%s%d" % (name, i)) for i in range(count)]

        f_scales = tiles("f_scales", [[P, PASSES, S_HALF]] * (S // S_HALF), U8)
        f_words = tiles("f_words", [[P, PASSES, F_CHUNK]] * (S // F_CHUNK), U32)
        a_raw = tiles("a_raw", [[P, PACK, N_TILE]] * PIECES, BF16)
        a_grouped = tiles("a_grouped", [[P, N_TILE * PACK]] * PASSES, BF16)
        a_codes = tiles("a_codes", [[P, N_TILE]] * PIECES, U32)
        a_scales = tiles("a_scales", [[P, N_TILE]] * PIECES, U8)
        wrench_sb = tiles("wrench", [[P, count, N_TILE] for g, j, count in units], BF16)
        y_sb = tiles("y", [[P, count * N_TILE] for g, j, count in units], F32)
        r_sb = tiles("r", [[P, PAIR * N_TILE]] * RING, F32)
        y_rounded = tiles("y_rounded", [[P, PAIR * N_TILE]] * RING, BF16)
        y_turned = tiles("y_turned", [[P, PAIR * N_TILE]] * TURNED_RING, BF16)
        y_codes = tiles("y_codes", [[P, S]] * GROUPS, U32)
        y_scales = tiles("y_scales", [[P, S]] * GROUPS, U8)
        weight_row = sb.tile([P, N], BF16, name="weight_row", align_bytes=64)
        ones_src = sb.tile([P, P], BF16, name="ones_src", align_bytes=64)
        ones = sb.tile([P, P], BF16, name="ones", align_bytes=64)
        ident = sb.tile([P, P], F32, name="ident", align_bytes=64)
        acc = banks("acc", ACC_BANKS)
        turn = banks("turn", TURN_BANKS)
        weight_bank = banks("weight_bank", WEIGHT_BANKS)


        def load_a(c):
            g, k = divmod(c, PASSES)
            rows = grasp_t[k * K_PASS : (k + 1) * K_PASS, g * N_TILE : (g + 1) * N_TILE]
            nc.sync.dma_start(out=a_raw[c][:], in_=rows.rearrange("(p t) n -> p t n", t=PACK))

        def load_f(q):
            cases = force_words.rearrange("k p s t -> p k (s t)")[:, :, q * F_CHUNK * PACK : (q + 1) * F_CHUNK * PACK]
            nc.sync.dma_start(out=f_words[q][:].bitcast(I32), in_=cases.bitcast(I32))

        def load_f_scales(half):
            rows = force_scales[:, :, half * S_HALF : (half + 1) * S_HALF].rearrange("k q s -> q k s")
            for r in range(SCALE_ROWS):
                nc.sync.dma_start(
                    out=f_scales[half][r:P:QUADRANT, :, :].bitcast(I32), in_=rows[r : 4 * SCALE_ROWS : SCALE_ROWS].bitcast(I32)
                )

        def load_wrench(u):
            g, j, count = units[u]
            rows = wrench[j * P : (j + count) * P, g * N_TILE : (g + 1) * N_TILE]
            nc.sync.dma_start(out=wrench_sb[u][:], in_=rows.rearrange("(j p) n -> p j n", p=P))

        for tile in f_scales:
            nc.vector.memset(tile[:].rearrange("p k s -> p (k s)").bitcast(I32), 0)
        nc.vector.memset(weight_row[:].bitcast(I32), 0)
        nc.vector.memset(ones_src[:], 1.0)
        make_identity(nc, ident[:])
        nc.scalar.activation(out=ones[:], in_=ones_src[:], func=ACT.Square)

        for c in range(PASSES):
            load_a(c)
        load_f_scales(0)
        load_f(0)
        load_wrench(0)
        nc.sync.dma_start(out=weight_row[0:1, :], in_=weight.rearrange("(o n) -> o n", o=1))
        load_a(PASSES)
        for u in range(1, len(units)):
            if u * F_CHUNK == S_HALF:
                load_f_scales(1)
            if u < len(f_words):
                load_f(u)
            load_wrench(u)
            if u + PASSES < PIECES:
                load_a(u + PASSES)


        def grouped(c):
            return a_grouped[min(c, PASSES - 1)]

        def interleave(engine_copy, c, lo, hi):
            engine_copy(
                out=grouped(c)[:, lo * PACK : hi * PACK].rearrange("p (c i t) -> p c t i", i=RUN, t=PACK),
                in_=a_raw[c][:, :, lo:hi].rearrange("p t (c i) -> p c t i", i=RUN),
            )

        def gpsimd_copy(out, in_):
            nc.gpsimd.tensor_scalar(out=out, in0=in_, scalar1=1.0, scalar2=0.0, op0=ALU.mult, op1=ALU.add)

        def interleave_gpsimd(c, lo):
            gpsimd_copy(
                out=grouped(c)[:, lo * PACK :].rearrange("p (c t) -> p c t", t=PACK),
                in_=a_raw[c][:, :, lo:].rearrange("p t c -> p c t"),
            )

        def vector_share(c):
            return VECTOR_SHARE if c >= PIECES - PASSES else 0

        def quantize_a(c):
            nc.vector.quantize_mx(out=a_codes[c][:].bitcast(E4M3X4), scales=a_scales[c][:], in_=grouped(c)[:])


        def acc_bank(u, jj):
            return acc[(first_tile[u] + jj) % ACC_BANKS]

        def mx_pass(u, jj, k):
            g, j, count = units[u]
            q, in_chunk = divmod((j + jj) * P, F_CHUNK)
            half, in_half = divmod((j + jj) * P, S_HALF)
            nc.tensor.matmul_mx(
                out=acc_bank(u, jj)[:],
                lhsT=f_words[q][:, k, in_chunk : in_chunk + P].bitcast(E5M2X4),
                lhsT_scale=f_scales[half][:, k, in_half : in_half + P],
                rhs=a_codes[g * PASSES + k][:].bitcast(E4M3X4),
                rhs_scale=a_scales[g * PASSES + k][:],
                start=(k == 0),
                stop=(k == PASSES - 1),
            )

        def product(u):
            for jj in range(units[u][2]):
                for k in range(PASSES):
                    mx_pass(u, jj, k)

        def product_passes(u, passes):
            for k in passes:
                for jj in range(units[u][2]):
                    mx_pass(u, jj, k)

        def spread_weight(g):
            nc.tensor.matmul(
                out=weight_bank[g % WEIGHT_BANKS][:],
                lhsT=ones[:],
                rhs=weight_row[:, g * N_TILE : (g + 1) * N_TILE],
                start=True,
                stop=True,
            )

        def subtract(u):
            for jj in range(units[u][2]):
                nc.vector.tensor_tensor(
                    out=r_sb[u % RING][:, jj * N_TILE : (jj + 1) * N_TILE],
                    in0=acc_bank(u, jj)[:],
                    in1=wrench_sb[u][:, jj, :],
                    op=ALU.subtract,
                )

        def square(u):
            nc.scalar.activation(out=y_sb[u][:], in_=r_sb[u % RING][:, : units[u][2] * N_TILE], func=ACT.Square)

        def weigh(u):
            g, j, count = units[u]
            y_tiles = y_sb[u][:].rearrange("p (j n) -> p j n", j=count)
            nc.vector.tensor_tensor(
                out=y_tiles,
                in0=y_tiles,
                in1=weight_bank[g % WEIGHT_BANKS][:].unsqueeze(1).to_broadcast([P, count, N_TILE]),
                op=ALU.mult,
            )
            rows = out_0[j * P : (j + count) * P, g * N_TILE : (g + 1) * N_TILE]
            nc.sync.dma_start(out=rows.rearrange("(j p) n -> p j n", p=P), in_=y_tiles)

        def round_y(u, engine_copy, halves=slice(0, 2)):
            width = units[u][2] * N_TILE
            engine_copy(
                out=y_rounded[u % RING][:, :width].rearrange("p (h m e) -> p h m e", h=2, e=2)[:, halves],
                in_=y_sb[u][:].rearrange("p (m h e) -> p h m e", h=2, e=2)[:, halves],
            )

        def round_shared(u):
            round_y(u, nc.scalar.copy, slice(0, 1))
            round_y(u, gpsimd_copy, slice(1, 2))

        def turn_bank(u):
            return acc[last - u] if u >= last - 1 else turn[u % TURN_BANKS]

        def turn_y(u):
            count = units[u][2]
            words = y_rounded[u % RING][:, : count * N_TILE].bitcast(F32)
            for b in range(2 * count):
                nc.tensor.transpose(turn_bank(u)[:, b * P : (b + 1) * P], words[:, b * P : (b + 1) * P], ident[:])

        def copy_turned(u):
            count = units[u][2]
            nc.scalar.copy(
                out=y_turned[u % TURNED_RING][:, : count * N_TILE].bitcast(F32).rearrange("p (s h) -> p s h", h=2),
                in_=turn_bank(u)[:, : 2 * count * P].rearrange("p (h s) -> p s h", h=2),
            )

        def quantize_y_tiles(u, lo, hi):
            g, j, count = units[u]
            cases = slice((j + lo) * P, (j + hi) * P)
            nc.vector.quantize_mx(
                out=y_codes[g][:, cases].bitcast(E4M3X4),
                scales=y_scales[g][:, cases],
                in_=y_turned[u % TURNED_RING][:, lo * N_TILE : hi * N_TILE],
            )

        def quantize_y(u):
            quantize_y_tiles(u, 0, units[u][2])

        def store_words(g, lo, hi):
            nc.sync.dma_start(
                out=out_1[g].rearrange("p s t -> p (s t)")[:, lo * PACK : hi * PACK].bitcast(I32),
                in_=y_codes[g][:, lo:hi].bitcast(I32),
            )

        def store_scales(g, queues):
            for r in range(SCALE_ROWS):
                queues[r % len(queues)].dma_start(
                    out=out_2[g, r : 4 * SCALE_ROWS : SCALE_ROWS, :].bitcast(I32),
                    in_=y_scales[g][r:P:QUADRANT, :].bitcast(I32),
                )

        for c in range(PASSES):
            interleave(nc.scalar.copy, c, EVEN_SHARE, N_TILE)
        interleave(nc.vector.tensor_copy, 0, 0, EVEN_SHARE)
        quantize_a(0)
        interleave(nc.vector.tensor_copy, 1, 0, EVEN_SHARE)
        for c in range(2, PASSES):
            interleave(nc.vector.tensor_copy, c, 0, EVEN_SHARE)
            quantize_a(c - 1)
        quantize_a(PASSES - 1)
        product(0)
        spread_weight(0)
        interleave(nc.scalar.copy, PASSES, EVEN_SHARE, N_TILE)

        for i in range(last - 1):
            c = i + PASSES
            opens_group = units[i + 1][1] == 0
            if i >= 2:
                if c - 1 < PIECES:
                    round_y(i - 2, nc.scalar.copy)
                else:
                    round_shared(i - 2)
            if opens_group:
                product_passes(i + 1, range(PASSES - 1))
            else:
                product(i + 1)
            if i >= 2:
                turn_y(i - 2)
            if opens_group:
                spread_weight(units[i + 1][0])
            subtract(i)
            if i == 0:
                interleave(nc.vector.tensor_copy, c, 0, EVEN_SHARE)
            shares_piece = c < PIECES and vector_share(c) > 0
            if shares_piece:
                interleave(nc.vector.tensor_copy, c, 0, vector_share(c))
            square(i)
            if shares_piece:
                quantize_y_tiles(i - 3, 0, 1)
            if c < PIECES:
                quantize_a(c)
            if opens_group:
                product_passes(i + 1, [PASSES - 1])
            if i >= 3:
                quantize_y_tiles(i - 3, 1 if shares_piece else 0, PAIR)
                if units[i - 3][1] + PAIR == CASE_TILES:
                    store_words(units[i - 3][0], 0, S)
                    store_scales(units[i - 3][0], [nc.sync])
            if c + 1 < PIECES:
                gpsimd_from = N_TILE - (GPSIMD_SHARE if i > 0 else GPSIMD_FIRST_SHARE)
                interleave_gpsimd(c + 1, gpsimd_from)
                interleave(nc.scalar.copy, c + 1, vector_share(c + 1), gpsimd_from)
            if i >= 2:
                copy_turned(i - 2)
            if i >= 1:
                weigh(i - 1)

        pair, single, final = last - 2, last - 1, last
        round_shared(pair - 1)
        product(final)
        turn_y(pair - 1)
        subtract(single)
        square(single)
        weigh(pair)
        round_shared(pair)
        subtract(final)
        square(final)
        copy_turned(pair - 1)
        turn_y(pair)
        weigh(single)
        round_y(single, nc.vector.tensor_copy)
        weigh(final)
        quantize_y(pair - 2)
        round_y(final, nc.vector.tensor_copy)
        for u in (single, final):
            turn_y(u)
        for u in (pair, single, final):
            copy_turned(u)
        quantize_y(pair - 1)
        quantize_y(pair)
        singles_from = units[single][1] * P
        store_words(GROUPS - 1, 0, singles_from)
        quantize_y(single)
        quantize_y(final)
        store_words(GROUPS - 1, singles_from, S)
        store_scales(GROUPS - 1, [nc.scalar, nc.sync])
